import numpy as np
import ml_dtypes


def mxq(x, axis, fmt="e4m3"):
    dtype, down = {"e4m3": (ml_dtypes.float8_e4m3fn, 7), "e5m2": (ml_dtypes.float8_e5m2, 14)}[fmt]
    v = np.moveaxis(np.asarray(x, np.float32).astype(ml_dtypes.bfloat16).astype(np.float64), axis, -1)
    blocks = v.reshape(v.shape[:-1] + (-1, 32))
    amax = np.abs(blocks).max(-1, keepdims=True)
    byte = np.maximum(np.where(amax > 0, np.frexp(amax)[1] - 1 + 127, 0) - down, 1)
    scale = np.exp2(byte - 127.0)
    codes = (blocks / scale).astype(np.float32).astype(dtype).astype(np.float64)
    return np.moveaxis((codes * scale).reshape(v.shape), -1, axis)


WIDE = False


def mx_kscale(k):
    if not WIDE:
        return np.ones(k)
    levels = np.array([10, -10, 5, -5, 0])
    if k % 512:
        return np.exp2(np.random.permutation(np.resize(levels, k // 32))).repeat(32)
    a = np.empty((k // 512, 16))
    for p in range(k // 512):
        a[p, :8] = np.random.permutation(np.resize(levels, 8))
        for g in range(8):
            far = levels[np.abs(levels - a[p, g]) >= 10]
            a[p, g + 8] = far[np.random.randint(len(far))]
    return np.exp2(a.ravel()).repeat(32)


def f64(x):
    return np.asarray(x).astype(np.float64)


def striped(idx):
    return np.tile(idx.reshape(-1, 16).T, (8, 1)).astype(np.uint16)


def unstriped(offs):
    return offs[:16].T.reshape(-1).astype(np.int64)


E2M1 = np.array([0.0, 0.5, 1.0, 1.5, 2.0, 3.0, 4.0, 6.0, -0.0, -0.5, -1.0, -1.5, -2.0, -3.0, -4.0, -6.0])


def pack_weight(w, fmt):
    k, n = w.shape
    w = f64(np.asarray(w, np.float32).astype(ml_dtypes.bfloat16)).reshape(k // 32, 32, n)
    amax = np.abs(w).max(1)
    if fmt == "e4m3":
        byte = np.frexp(amax)[1] - 1 + 127 - 7
    else:
        mant, ex = np.frexp(amax / 6.0)
        byte = np.where(mant > 0.5, ex, ex - 1) + 127
    byte = np.clip(np.where(amax > 0, byte, 1), 1, 254)
    scaled = (w * np.exp2(127.0 - byte)[:, None, :]).reshape(k, n).astype(np.float32)
    by_word = np.ascontiguousarray(scaled.reshape(k // 512, 128, 4, n).transpose(0, 1, 3, 2))
    if fmt == "e4m3":
        words = by_word.astype(ml_dtypes.float8_e4m3fn).view(np.uint8)
    else:
        c = by_word.astype(ml_dtypes.float4_e2m1fn).view(np.uint8) & 0xF
        words = (c[..., 0::2] | (c[..., 1::2] << 4)).reshape(k // 512, 128, 2 * n)
    return np.ascontiguousarray(words), np.ascontiguousarray(byte.astype(np.uint8).reshape(k // 512, 16, n))


def unpack_weight(words, scales, fmt):
    g, _, n = scales.shape
    words = np.ascontiguousarray(words).reshape(g, 128, n, -1)
    if fmt == "e4m3":
        vals = words.view(ml_dtypes.float8_e4m3fn).astype(np.float64)
    else:
        nib = np.empty((g, 128, n, 4), np.uint8)
        nib[..., 0::2] = words & 0xF
        nib[..., 1::2] = words >> 4
        vals = E2M1[nib]
    vals = vals * np.repeat(np.exp2(scales.astype(np.float64) - 127.0), 8, axis=1)[..., None]
    return vals.transpose(0, 1, 3, 2).reshape(g * 512, n)


def gelu(v):
    return 0.5 * v * (1.0 + np.tanh(np.sqrt(2.0 / np.pi) * (v + 0.044715 * v**3)))


K, H, T, S, T3, S2, P = 1024, 512, 4096, 1024, 2048, 1024, 512

def setup_inputs():
    n = np.random.standard_normal
    s = mx_kscale(K)[:, None]
    u = mx_kscale(H)[:, None]
    tab_words, tab_scales = pack_weight(n((K, T)) * s, "e4m3")
    tab2_words, tab2_scales = pack_weight(n((H, T3)) / np.sqrt(H) / u, "e4m3")
    w3_words, w3_scales = pack_weight(n((K, H)) / np.sqrt(K) / s, "e2m1")
    return {
        "tab_words": tab_words, "tab_scales": tab_scales,
        "offs": striped(np.random.permutation(T)[:S]),
        "tab2_words": tab2_words, "tab2_scales": tab2_scales,
        "offs2": striped(np.random.permutation(T3)[:S2]),
        "pos1": striped(np.random.permutation(S)[:P]),
        "pos2": striped(np.random.permutation(S)[:P]),
        "w1": (n((K, H)) / np.sqrt(K) / s).astype(np.float32),
        "w2": (n((K, H)) / np.sqrt(K) / s).astype(np.float32),
        "w3_words": w3_words, "w3_scales": w3_scales,
        "chan": (np.exp(0.3 * n(H)) * u[:, 0]).astype(np.float32),
        "lift": np.random.uniform(3.0, 7.0, S2).astype(np.float32),
        "mat": n((S2, P)).astype(np.float32),
    }

def reference(tab_words, tab_scales, offs, tab2_words, tab2_scales, offs2, pos1, pos2,
              w1, w2, w3_words, w3_scales, chan, lift, mat):
    v = unpack_weight(tab_words, tab_scales, "e4m3")[:, unstriped(offs)]
    v2 = unpack_weight(tab2_words, tab2_scales, "e4m3")[:, unstriped(offs2)]
    r1 = mxq(f64(w1), 0, "e4m3").T @ v
    r2 = mxq(f64(w2), 0, "e4m3").T @ v
    r3 = unpack_weight(w3_words, w3_scales, "e2m1").T @ v
    h = f64(chan)[:, None] * np.tanh(np.maximum(r1, r2) + r3)
    e = v2.T @ mxq(h, 0, "e4m3")
    top = e.max(axis=1)
    a = np.exp(e[:, unstriped(pos1)] - top[:, None])
    c = e[:, unstriped(pos2)]
    return (f64(lift)[:, None] * a + c) * f64(mat)

@@ -1,0 +1,220 @@
+from contextlib import ExitStack
+
+import concourse.mybir as mybir
+from concourse.masks import make_identity
+
+K, H, T, S, T3, S2, NP = 1024, 512, 4096, 1024, 2048, 1024, 512
+FLOPS = 3 * 2 * K * H * S + 2 * H * S2 * S
+
+F32 = mybir.dt.float32
+BF16 = mybir.dt.bfloat16
+I32 = mybir.dt.int32
+U32 = mybir.dt.uint32
+U16 = mybir.dt.uint16
+U8 = mybir.dt.uint8
+FP8X4 = mybir.dt.float8_e4m3fn_x4
+FP4X4 = mybir.dt.float4_e2m1fn_x4
+ALU = mybir.AluOpType
+ACT = mybir.ActivationFunctionType
+
+P = 128
+PACK = 4
+PASSES = K // (P * PACK)
+CHUNKS = S // P
+GOODS = S2 // P
+HALF = 512
+
+
+def tile_list_tariff_ruling_scores_kernel(
+    tc, tab_words, tab_scales, offs, tab2_words, tab2_scales, offs2, pos1, pos2,
+    w1, w2, w3_words, w3_scales, chan, lift, mat, out,
+):
+    nc = tc.nc
+    with ExitStack() as ctx:
+        keep = ctx.enter_context(tc.tile_pool(name="keep", bufs=1))
+        ring2 = ctx.enter_context(tc.tile_pool(name="ring2", bufs=2))
+        ring3 = ctx.enter_context(tc.tile_pool(name="ring3", bufs=3))
+        ring4 = ctx.enter_context(tc.tile_pool(name="ring4", bufs=4))
+        mm = ctx.enter_context(tc.psum_pool(name="mm", bufs=4))
+        xs = ctx.enter_context(tc.psum_pool(name="xs", bufs=4))
+
+        offs_t = keep.tile([P, S // 16], U16, name="offs_t")
+        offs2_t = keep.tile([P, S2 // 16], U16, name="offs2_t")
+        pos1_t = keep.tile([P, NP // 16], U16, name="pos1_t")
+        pos2_t = keep.tile([P, NP // 16], U16, name="pos2_t")
+        tab_sc = keep.tile([P, T], U8, name="tab_sc", align_bytes=64)
+        tab2_sc = keep.tile([P, T3], U8, name="tab2_sc", align_bytes=64)
+        tab_w = [keep.tile([P, T], I32, name=f"tab_w{a}", align_bytes=64) for a in range(PASSES)]
+        tab2_w = keep.tile([P, T3], I32, name="tab2_w", align_bytes=64)
+        w3_w = keep.tile([P, PASSES, 2 * H], U8, name="w3_w", align_bytes=64)
+        w3_pl = keep.tile([P, PASSES, H], U8, name="w3_pl", align_bytes=64)
+        v_pl = [keep.tile([P, S], U8, name=f"v_pl{a}", align_bytes=64) for a in range(PASSES)]
+        v2_pl = keep.tile([P, S2], U8, name="v2_pl", align_bytes=64)
+        v_sc = keep.tile([P, S], U8, name="v_sc", align_bytes=64)
+        v2_sc = keep.tile([P, S2], U8, name="v2_sc", align_bytes=64)
+        v_w = [keep.tile([P, S], U32, name=f"v_w{a}", align_bytes=64) for a in range(PASSES)]
+        v2_w = keep.tile([P, S2], U32, name="v2_w", align_bytes=64)
+        ident = keep.tile([P, P], F32, name="ident", align_bytes=64)
+        chan_t = keep.tile([P, PACK], F32, name="chan_t")
+        lift_t = keep.tile([P, GOODS], F32, name="lift_t")
+
+        SC0 = P - 16 * PASSES
+        SC2 = P - 16
+        nc.vector.memset(tab_sc[0:SC0, :].bitcast(I32), 0)
+        nc.vector.memset(tab2_sc[0:SC2, :].bitcast(I32), 0)
+        nc.gpsimd.memset(w3_pl[:].rearrange("p a c -> p (a c)").bitcast(I32), 0)
+        for a in range(PASSES):
+            nc.gpsimd.memset(v_pl[a][:].bitcast(I32), 0)
+        nc.gpsimd.memset(v2_pl[:].bitcast(I32), 0)
+        make_identity(nc, ident[:])
+
+        nc.sync.dma_start(offs_t[:], offs)
+        nc.sync.dma_start(tab_sc[SC0:P, :].bitcast(I32), tab_scales.rearrange("a q t -> (a q) t").bitcast(I32))
+        nc.sync.dma_start(offs2_t[:], offs2)
+        nc.sync.dma_start(tab2_sc[SC2:P, :].bitcast(I32), tab2_scales[0].bitcast(I32))
+        for a in range(PASSES):
+            nc.sync.dma_start(tab_w[a][:], tab_words[a].rearrange("p t i -> p (t i)").bitcast(I32))
+        nc.sync.dma_start(w3_w[:].bitcast(I32), w3_words.rearrange("a p c -> p a c").bitcast(I32))
+        for q in range(4):
+            nc.gpsimd.dma_start(
+                w3_pl[32 * q : 32 * q + 4, :, :].bitcast(I32),
+                w3_scales[:, 4 * q : 4 * q + 4, :].rearrange("a r c -> r a c").bitcast(I32),
+            )
+
+        def load_w(w, a, c0, c1, name):
+            raw = keep.tile([P, PACK, c1 - c0], F32, name=name, align_bytes=64)
+            nc.sync.dma_start(raw[:], w[512 * a : 512 * (a + 1), c0:c1].rearrange("(p i) c -> p i c", i=PACK))
+            return raw
+
+        w1_raw = [load_w(w1, a, 0, H, f"w1_raw{a}") for a in range(PASSES)]
+        nc.sync.dma_start(tab2_w[:], tab2_words[0].rearrange("p t i -> p (t i)").bitcast(I32))
+        w2_raw0 = load_w(w2, 0, 0, H, "w2_raw0")
+        nc.sync.dma_start(chan_t[:], chan.rearrange("(p i) -> p i", i=PACK))
+        w2_raw1 = [load_w(w2, 1, c * 256, (c + 1) * 256, f"w2_raw1_{c}") for c in range(2)]
+        nc.sync.dma_start(pos1_t[:], pos1)
+        nc.sync.dma_start(pos2_t[:], pos2)
+        with nc.allow_non_contiguous_dma(reason="one value of lift a partition and tile"):
+            nc.sync.dma_start(lift_t[:], lift.rearrange("(g p) -> p g", p=P))
+        mat_t = []
+        for g in range(GOODS):
+            m_t = keep.tile([P, NP], F32, name=f"mat{g}", align_bytes=64)
+            nc.sync.dma_start(m_t[:], mat[g * P : (g + 1) * P, :])
+            mat_t.append(m_t)
+
+        nc.vector.tensor_copy(v_sc[:], tab_sc[:].indirect(offs_t[:]))
+        for a in range(PASSES):
+            for q in range(4):
+                r0 = SC0 + 16 * a + 4 * q
+                nc.gpsimd.dma_start(v_pl[a][32 * q : 32 * q + 4, :].bitcast(I32), v_sc[r0 : r0 + 4, :].bitcast(I32))
+        nc.vector.tensor_copy(v2_sc[:], tab2_sc[:].indirect(offs2_t[:]))
+        nc.vector.tensor_copy(v_w[0][:], tab_w[0][:].bitcast(U32).indirect(offs_t[:]))
+        for hf in range(2):
+            nc.vector.tensor_copy(
+                v_w[1][:, hf * HALF : (hf + 1) * HALF],
+                tab_w[1][:].bitcast(U32).indirect(offs_t[:, hf * 32 : (hf + 1) * 32]),
+            )
+        for q in range(4):
+            r0 = SC2 + 4 * q
+            nc.gpsimd.dma_start(v2_pl[32 * q : 32 * q + 4, :].bitcast(I32), v2_sc[r0 : r0 + 4, :].bitcast(I32))
+
+        def quantise_w(raw, codes, plane, width):
+            grouped = ring2.tile([P, width, PACK], BF16, name=f"grouped{width}", align_bytes=64)
+            nc.vector.tensor_copy(
+                grouped[:].rearrange("p (c u) i -> p c i u", u=4),
+                raw[:].rearrange("p i (c u) -> p c i u", u=4),
+            )
+            nc.vector.quantize_mx(out=codes.bitcast(FP8X4), scales=plane, in_=grouped[:].rearrange("p c i -> p (c i)"))
+
+        w_codes = {}
+        w_plane = {}
+        for name in ("w1", "w2"):
+            for a in range(PASSES):
+                w_codes[name, a] = keep.tile([P, H], U32, name=f"{name}_c{a}", align_bytes=64)
+                w_plane[name, a] = keep.tile([P, H], U8, name=f"{name}_p{a}", align_bytes=64)
+
+        def product(c, rhs, rhs_pl):
+            acc = mm.tile([P, H], F32, name="acc")
+            cols = slice(c * P, (c + 1) * P)
+            for a in range(PASSES):
+                nc.tensor.matmul_mx(
+                    out=acc[:], lhsT=v_w[a][:, cols].bitcast(FP8X4), lhsT_scale=v_pl[a][:, cols],
+                    rhs=rhs[a], rhs_scale=rhs_pl[a], start=(a == 0), stop=(a == PASSES - 1),
+                )
+            return acc
+
+        def dealt(acc):
+            return acc[:].rearrange("j (p i) -> j i p", i=PACK)
+
+        r3 = []
+        for c in range(CHUNKS):
+            acc = product(c, [w3_w[:, a, :].bitcast(FP4X4) for a in range(PASSES)], [w3_pl[:, a, :] for a in range(PASSES)])
+            r_sb = keep.tile([P, PACK, P], F32, name=f"r3_{c}", align_bytes=64)
+            nc.scalar.copy(r_sb[:], dealt(acc))
+            r3.append(r_sb)
+
+        for a in range(PASSES):
+            quantise_w(w1_raw[a], w_codes["w1", a][:], w_plane["w1", a][:], H)
+        nc.vector.tensor_copy(v2_w[:], tab2_w[:].bitcast(U32).indirect(offs2_t[:]))
+
+        r1 = []
+        for c in range(CHUNKS):
+            acc = product(c, [w_codes["w1", a][:].bitcast(FP8X4) for a in range(PASSES)], [w_plane["w1", a][:] for a in range(PASSES)])
+            r_sb = keep.tile([P, PACK, P], F32, name=f"r1_{c}", align_bytes=64)
+            nc.scalar.copy(r_sb[:], dealt(acc))
+            r1.append(r_sb)
+
+        quantise_w(w2_raw0, w_codes["w2", 0][:], w_plane["w2", 0][:], H)
+        for c in range(2):
+            cols = slice(c * 256, (c + 1) * 256)
+            quantise_w(w2_raw1[c], w_codes["w2", 1][:, cols], w_plane["w2", 1][:, cols], 256)
+
+        h_codes = [keep.tile([P, HALF], U32, name=f"h_c{b}", align_bytes=64) for b in range(2)]
+        h_plane = [keep.tile([P, HALF], U8, name=f"h_p{b}", align_bytes=64) for b in range(2)]
+        chan_b = chan_t[:].unsqueeze(1).to_broadcast([P, P, PACK])
+        for c in range(CHUNKS):
+            acc = product(c, [w_codes["w2", a][:].bitcast(FP8X4) for a in range(PASSES)], [w_plane["w2", a][:] for a in range(PASSES)])
+            y = ring3.tile([P, PACK, P], F32, name="y", align_bytes=64)
+            nc.vector.tensor_tensor(y[:], dealt(acc), r1[c][:], ALU.max)
+            x = xs.tile([P, PACK, P], F32, name="x")
+            for i in range(PACK):
+                nc.tensor.matmul(x[:, i, :], lhsT=r3[c][:, i, :], rhs=ident[:], is_transpose=True, start=(i == 0), stop=False)
+            for i in range(PACK):
+                nc.tensor.matmul(x[:, i, :], lhsT=y[:, i, :], rhs=ident[:], is_transpose=True, start=False, stop=(i == PACK - 1))
+            th = ring3.tile([P, P, PACK], F32, name="th", align_bytes=64)
+            nc.scalar.activation(out=th[:], in_=x[:].rearrange("p i j -> p j i"), func=ACT.Tanh)
+            hb = ring3.tile([P, P, PACK], BF16, name="hb", align_bytes=64)
+            nc.vector.tensor_tensor(hb[:], th[:], chan_b, ALU.mult)
+            b, cols = c // 4, slice((c % 4) * P, (c % 4 + 1) * P)
+            nc.vector.quantize_mx(
+                out=h_codes[b][:, cols].bitcast(FP8X4), scales=h_plane[b][:, cols],
+                in_=hb[:].rearrange("p j i -> p (j i)"),
+            )
+
+        for g in range(GOODS):
+            rows = slice(g * P, (g + 1) * P)
+            e = ring4.tile([P, S], F32, name="e", align_bytes=64)
+            mx = ring4.tile([P, 2], F32, name="mx")
+            for b in range(2):
+                acc = mm.tile([P, HALF], F32, name="acc")
+                nc.tensor.matmul_mx(
+                    out=acc[:], lhsT=v2_w[:, rows].bitcast(FP8X4), lhsT_scale=v2_pl[:, rows],
+                    rhs=h_codes[b][:].bitcast(FP8X4), rhs_scale=h_plane[b][:], start=True, stop=True,
+                )
+                nc.vector.tensor_scalar(
+                    out=e[:, b * HALF : (b + 1) * HALF], in0=acc[:], scalar1=1.0, scalar2=None,
+                    op0=ALU.mult, op1=ALU.max, accum_out=mx[:, b : b + 1],
+                )
+            nt = ring4.tile([P, 1], F32, name="nt")
+            nc.vector.tensor_scalar(out=nt[:], in0=mx[:, 0:1], scalar1=mx[:, 1:2], scalar2=-1.0, op0=ALU.max, op1=ALU.mult)
+            a_t = ring3.tile([P, NP], F32, name="a_t", align_bytes=64)
+            nc.scalar.activation(out=a_t[:], in_=e[:].indirect(pos1_t[:]), func=ACT.Exp, bias=nt[:])
+            c_t = ring3.tile([P, NP], F32, name="c_t", align_bytes=64)
+            nc.vector.tensor_copy(c_t[:], e[:].indirect(pos2_t[:]))
+            if g < GOODS - 1:
+                nc.scalar.activation(out=a_t[:], in_=a_t[:], func=ACT.Copy, scale=lift_t[:, g : g + 1])
+                nc.gpsimd.tensor_tensor(c_t[:], a_t[:], c_t[:], ALU.add)
+                nc.gpsimd.tensor_tensor(mat_t[g][:], c_t[:], mat_t[g][:], ALU.mult)
+            else:
+                nc.vector.scalar_tensor_tensor(c_t[:], a_t[:], lift_t[:, g : g + 1], c_t[:], ALU.mult, ALU.add)
+                nc.vector.tensor_tensor(mat_t[g][:], c_t[:], mat_t[g][:], ALU.mult)
+            nc.sync.dma_start(out[rows, :], mat_t[g][:])

@@ -42,15 +42,15 @@ def tile_list_tariff_ruling_scores_kernel(
         offs2_t = keep.tile([P, S2 // 16], U16, name="offs2_t")
         pos1_t = keep.tile([P, NP // 16], U16, name="pos1_t")
         pos2_t = keep.tile([P, NP // 16], U16, name="pos2_t")
-        tab_sc = keep.tile([P, T], U8, name="tab_sc", align_bytes=64)
+        tab_sc = keep.tile([P, PASSES, T], U8, name="tab_sc", align_bytes=64)
+        v_sc = keep.tile([P, PASSES, S], U8, name="v_sc", align_bytes=64)
         tab2_sc = keep.tile([P, T3], U8, name="tab2_sc", align_bytes=64)
         tab_w = [keep.tile([P, T], I32, name=f"tab_w{a}", align_bytes=64) for a in range(PASSES)]
         tab2_w = keep.tile([P, T3], I32, name="tab2_w", align_bytes=64)
         w3_w = keep.tile([P, PASSES, 2 * H], U8, name="w3_w", align_bytes=64)
         w3_pl = keep.tile([P, PASSES, H], U8, name="w3_pl", align_bytes=64)
-        v_pl = [keep.tile([P, S], U8, name=f"v_pl{a}", align_bytes=64) for a in range(PASSES)]
+        v_pl = keep.tile([P, PASSES, S], U8, name="v_pl", align_bytes=64)
         v2_pl = keep.tile([P, S2], U8, name="v2_pl", align_bytes=64)
-        v_sc = keep.tile([P, S], U8, name="v_sc", align_bytes=64)
         v2_sc = keep.tile([P, S2], U8, name="v2_sc", align_bytes=64)
         v_w = [keep.tile([P, S], U32, name=f"v_w{a}", align_bytes=64) for a in range(PASSES)]
         v2_w = keep.tile([P, S2], U32, name="v2_w", align_bytes=64)
@@ -58,40 +58,52 @@ def tile_list_tariff_ruling_scores_kernel(
         chan_t = keep.tile([P, PACK], F32, name="chan_t")
         lift_t = keep.tile([P, GOODS], F32, name="lift_t")
 
-        SC0 = P - 16 * PASSES
         SC2 = P - 16
-        nc.vector.memset(tab_sc[0:SC0, :].bitcast(I32), 0)
+        nc.vector.memset(tab_sc[0:SC2, :, :].rearrange("p a t -> p (a t)").bitcast(I32), 0)
         nc.vector.memset(tab2_sc[0:SC2, :].bitcast(I32), 0)
         nc.gpsimd.memset(w3_pl[:].rearrange("p a c -> p (a c)").bitcast(I32), 0)
-        for a in range(PASSES):
-            nc.gpsimd.memset(v_pl[a][:].bitcast(I32), 0)
+        nc.gpsimd.memset(v_pl[:].rearrange("p a t -> p (a t)").bitcast(I32), 0)
         nc.gpsimd.memset(v2_pl[:].bitcast(I32), 0)
         make_identity(nc, ident[:])
-
-        nc.sync.dma_start(offs_t[:], offs)
-        nc.sync.dma_start(tab_sc[SC0:P, :].bitcast(I32), tab_scales.rearrange("a q t -> (a q) t").bitcast(I32))
-        nc.sync.dma_start(offs2_t[:], offs2)
-        nc.sync.dma_start(tab2_sc[SC2:P, :].bitcast(I32), tab2_scales[0].bitcast(I32))
-        for a in range(PASSES):
-            nc.sync.dma_start(tab_w[a][:], tab_words[a].rearrange("p t i -> p (t i)").bitcast(I32))
-        nc.sync.dma_start(w3_w[:].bitcast(I32), w3_words.rearrange("a p c -> p a c").bitcast(I32))
-        for q in range(4):
-            nc.gpsimd.dma_start(
-                w3_pl[32 * q : 32 * q + 4, :, :].bitcast(I32),
-                w3_scales[:, 4 * q : 4 * q + 4, :].rearrange("a r c -> r a c").bitcast(I32),
-            )
 
         def load_w(w, a, c0, c1, name):
             raw = keep.tile([P, PACK, c1 - c0], F32, name=name, align_bytes=64)
             nc.sync.dma_start(raw[:], w[512 * a : 512 * (a + 1), c0:c1].rearrange("(p i) c -> p i c", i=PACK))
             return raw
 
-        w1_raw = [load_w(w1, a, 0, H, f"w1_raw{a}") for a in range(PASSES)]
+        def load_words(a):
+            nc.sync.dma_start(tab_w[a][:], tab_words[a].rearrange("p t i -> p (t i)").bitcast(I32))
+
+        def move_rows(plane, gathered):
+            for q in range(4):
+                nc.sync.dma_start(
+                    plane[32 * q : 32 * q + 4, :].bitcast(I32), gathered[SC2 + 4 * q : SC2 + 4 * q + 4, :].bitcast(I32)
+                )
+
+        nc.sync.dma_start(offs_t[:], offs)
+        nc.sync.dma_start(tab_sc[SC2:P, :, :].bitcast(I32), tab_scales.rearrange("a q t -> q a t").bitcast(I32))
+        nc.sync.dma_start(offs2_t[:], offs2)
+        nc.sync.dma_start(tab2_sc[SC2:P, :].bitcast(I32), tab2_scales[0].bitcast(I32))
+        nc.sync.dma_start(w3_w[:].bitcast(I32), w3_words.rearrange("a p c -> p a c").bitcast(I32))
+        load_words(0)
+        nc.sync.dma_start(chan_t[:], chan.rearrange("(p i) -> p i", i=PACK))
+        nc.sync.dma_start(pos1_t[:], pos1)
+        for q in range(4):
+            nc.sync.dma_start(
+                w3_pl[32 * q : 32 * q + 4, :, :].bitcast(I32),
+                w3_scales[:, 4 * q : 4 * q + 4, :].rearrange("a r c -> r a c").bitcast(I32),
+            )
+        load_words(1)
+        for a in range(PASSES):
+            nc.vector.tensor_copy(v_sc[:, a, :], tab_sc[:, a, :].indirect(offs_t[:]))
+        move_rows(v_pl[:].rearrange("p a t -> p (a t)"), v_sc[:].rearrange("p a t -> p (a t)"))
+        w1_raw = [load_w(w1, 0, 0, H, "w1_raw0")]
+        w1_raw.append(load_w(w1, 1, 0, H, "w1_raw1"))
         nc.sync.dma_start(tab2_w[:], tab2_words[0].rearrange("p t i -> p (t i)").bitcast(I32))
         w2_raw0 = load_w(w2, 0, 0, H, "w2_raw0")
-        nc.sync.dma_start(chan_t[:], chan.rearrange("(p i) -> p i", i=PACK))
         w2_raw1 = [load_w(w2, 1, c * 256, (c + 1) * 256, f"w2_raw1_{c}") for c in range(2)]
-        nc.sync.dma_start(pos1_t[:], pos1)
+        nc.vector.tensor_copy(v2_sc[:], tab2_sc[:].indirect(offs2_t[:]))
+        move_rows(v2_pl[:], v2_sc[:])
         nc.sync.dma_start(pos2_t[:], pos2)
         with nc.allow_non_contiguous_dma(reason="one value of lift a partition and tile"):
             nc.sync.dma_start(lift_t[:], lift.rearrange("(g p) -> p g", p=P))
@@ -101,25 +113,16 @@ def tile_list_tariff_ruling_scores_kernel(
             nc.sync.dma_start(m_t[:], mat[g * P : (g + 1) * P, :])
             mat_t.append(m_t)
 
-        nc.vector.tensor_copy(v_sc[:], tab_sc[:].indirect(offs_t[:]))
-        for a in range(PASSES):
-            for q in range(4):
-                r0 = SC0 + 16 * a + 4 * q
-                nc.gpsimd.dma_start(v_pl[a][32 * q : 32 * q + 4, :].bitcast(I32), v_sc[r0 : r0 + 4, :].bitcast(I32))
-        nc.vector.tensor_copy(v2_sc[:], tab2_sc[:].indirect(offs2_t[:]))
         nc.vector.tensor_copy(v_w[0][:], tab_w[0][:].bitcast(U32).indirect(offs_t[:]))
         for hf in range(2):
             nc.vector.tensor_copy(
                 v_w[1][:, hf * HALF : (hf + 1) * HALF],
                 tab_w[1][:].bitcast(U32).indirect(offs_t[:, hf * 32 : (hf + 1) * 32]),
             )
-        for q in range(4):
-            r0 = SC2 + 4 * q
-            nc.gpsimd.dma_start(v2_pl[32 * q : 32 * q + 4, :].bitcast(I32), v2_sc[r0 : r0 + 4, :].bitcast(I32))
 
-        def quantise_w(raw, codes, plane, width):
-            grouped = ring2.tile([P, width, PACK], BF16, name=f"grouped{width}", align_bytes=64)
-            nc.vector.tensor_copy(
+        def quantise_w(raw, codes, plane, width, copy=nc.vector.tensor_copy):
+            grouped = ring2.tile([P, width, PACK], BF16, name="grouped", align_bytes=64)
+            copy(
                 grouped[:].rearrange("p (c u) i -> p c i u", u=4),
                 raw[:].rearrange("p i (c u) -> p c i u", u=4),
             )
@@ -132,19 +135,20 @@ def tile_list_tariff_ruling_scores_kernel(
                 w_codes[name, a] = keep.tile([P, H], U32, name=f"{name}_c{a}", align_bytes=64)
                 w_plane[name, a] = keep.tile([P, H], U8, name=f"{name}_p{a}", align_bytes=64)
 
-        def product(c, rhs, rhs_pl):
+        def product(c, rhs, rhs_pl, order=(0, 1)):
             acc = mm.tile([P, H], F32, name="acc")
             cols = slice(c * P, (c + 1) * P)
-            for a in range(PASSES):
+            for a in order:
                 nc.tensor.matmul_mx(
-                    out=acc[:], lhsT=v_w[a][:, cols].bitcast(FP8X4), lhsT_scale=v_pl[a][:, cols],
-                    rhs=rhs[a], rhs_scale=rhs_pl[a], start=(a == 0), stop=(a == PASSES - 1),
+                    out=acc[:], lhsT=v_w[a][:, cols].bitcast(FP8X4), lhsT_scale=v_pl[:, a, cols],
+                    rhs=rhs[a], rhs_scale=rhs_pl[a], start=(a == order[0]), stop=(a == order[-1]),
                 )
             return acc
 
         def dealt(acc):
             return acc[:].rearrange("j (p i) -> j i p", i=PACK)
 
+        quantise_w(w1_raw[0], w_codes["w1", 0][:], w_plane["w1", 0][:], H)
         r3 = []
         for c in range(CHUNKS):
             acc = product(c, [w3_w[:, a, :].bitcast(FP4X4) for a in range(PASSES)], [w3_pl[:, a, :] for a in range(PASSES)])
@@ -152,8 +156,7 @@ def tile_list_tariff_ruling_scores_kernel(
             nc.scalar.copy(r_sb[:], dealt(acc))
             r3.append(r_sb)
 
-        for a in range(PASSES):
-            quantise_w(w1_raw[a], w_codes["w1", a][:], w_plane["w1", a][:], H)
+        quantise_w(w1_raw[1], w_codes["w1", 1][:], w_plane["w1", 1][:], H)
         nc.vector.tensor_copy(v2_w[:], tab2_w[:].bitcast(U32).indirect(offs2_t[:]))
 
         r1 = []
@@ -170,12 +173,23 @@ def tile_list_tariff_ruling_scores_kernel(
 
         h_codes = [keep.tile([P, HALF], U32, name=f"h_c{b}", align_bytes=64) for b in range(2)]
         h_plane = [keep.tile([P, HALF], U8, name=f"h_p{b}", align_bytes=64) for b in range(2)]
+        e_t = [keep.tile([P, S], F32, name=f"e{g}", align_bytes=64) for g in range(GOODS)]
+
+        def scores(g, b):
+            rows = slice(g * P, (g + 1) * P)
+            acc = mm.tile([P, HALF], F32, name="acc")
+            nc.tensor.matmul_mx(
+                out=acc[:], lhsT=v2_w[:, rows].bitcast(FP8X4), lhsT_scale=v2_pl[:, rows],
+                rhs=h_codes[b][:].bitcast(FP8X4), rhs_scale=h_plane[b][:], start=True, stop=True,
+            )
+            nc.scalar.copy(e_t[g][:, b * HALF : (b + 1) * HALF], acc[:])
+
         chan_b = chan_t[:].unsqueeze(1).to_broadcast([P, P, PACK])
         for c in range(CHUNKS):
-            acc = product(c, [w_codes["w2", a][:].bitcast(FP8X4) for a in range(PASSES)], [w_plane["w2", a][:] for a in range(PASSES)])
+            acc = product(c, [w_codes["w2", a][:].bitcast(FP8X4) for a in range(PASSES)], [w_plane["w2", a][:] for a in range(PASSES)], (1, 0))
             y = ring3.tile([P, PACK, P], F32, name="y", align_bytes=64)
             nc.vector.tensor_tensor(y[:], dealt(acc), r1[c][:], ALU.max)
-            x = xs.tile([P, PACK, P], F32, name="x")
+            x = xs.tile([P, PACK, P], F32, name="x", tag="bank")
             for i in range(PACK):
                 nc.tensor.matmul(x[:, i, :], lhsT=r3[c][:, i, :], rhs=ident[:], is_transpose=True, start=(i == 0), stop=False)
             for i in range(PACK):
@@ -190,31 +204,21 @@ def tile_list_tariff_ruling_scores_kernel(
                 in_=hb[:].rearrange("p j i -> p (j i)"),
             )
 
+
         for g in range(GOODS):
             rows = slice(g * P, (g + 1) * P)
-            e = ring4.tile([P, S], F32, name="e", align_bytes=64)
-            mx = ring4.tile([P, 2], F32, name="mx")
-            for b in range(2):
-                acc = mm.tile([P, HALF], F32, name="acc")
-                nc.tensor.matmul_mx(
-                    out=acc[:], lhsT=v2_w[:, rows].bitcast(FP8X4), lhsT_scale=v2_pl[:, rows],
-                    rhs=h_codes[b][:].bitcast(FP8X4), rhs_scale=h_plane[b][:], start=True, stop=True,
-                )
-                nc.vector.tensor_scalar(
-                    out=e[:, b * HALF : (b + 1) * HALF], in0=acc[:], scalar1=1.0, scalar2=None,
-                    op0=ALU.mult, op1=ALU.max, accum_out=mx[:, b : b + 1],
-                )
+            e = e_t[g]
+            scores(g, 0)
+            scores(g, 1)
             nt = ring4.tile([P, 1], F32, name="nt")
-            nc.vector.tensor_scalar(out=nt[:], in0=mx[:, 0:1], scalar1=mx[:, 1:2], scalar2=-1.0, op0=ALU.max, op1=ALU.mult)
+            nc.vector.tensor_reduce(out=nt[:], in_=e[:], axis=mybir.AxisListType.X, op=ALU.max, negate=True)
             a_t = ring3.tile([P, NP], F32, name="a_t", align_bytes=64)
             nc.scalar.activation(out=a_t[:], in_=e[:].indirect(pos1_t[:]), func=ACT.Exp, bias=nt[:])
+            nc.scalar.activation(out=a_t[:], in_=a_t[:], func=ACT.Copy, scale=lift_t[:, g : g + 1])
             c_t = ring3.tile([P, NP], F32, name="c_t", align_bytes=64)
-            nc.vector.tensor_copy(c_t[:], e[:].indirect(pos2_t[:]))
-            if g < GOODS - 1:
-                nc.scalar.activation(out=a_t[:], in_=a_t[:], func=ACT.Copy, scale=lift_t[:, g : g + 1])
-                nc.gpsimd.tensor_tensor(c_t[:], a_t[:], c_t[:], ALU.add)
-                nc.gpsimd.tensor_tensor(mat_t[g][:], c_t[:], mat_t[g][:], ALU.mult)
-            else:
-                nc.vector.scalar_tensor_tensor(c_t[:], a_t[:], lift_t[:, g : g + 1], c_t[:], ALU.mult, ALU.add)
-                nc.vector.tensor_tensor(mat_t[g][:], c_t[:], mat_t[g][:], ALU.mult)
-            nc.sync.dma_start(out[rows, :], mat_t[g][:])
+            nc.vector.tensor_tensor(c_t[:], e[:].indirect(pos2_t[:]), a_t[:], ALU.add)
+            parts = 2 if g == GOODS - 1 else 1
+            for part in range(parts):
+                cols = slice(part * NP // parts, (part + 1) * NP // parts)
+                nc.vector.tensor_tensor(mat_t[g][:, cols], c_t[:, cols], mat_t[g][:, cols], ALU.mult)
+                nc.sync.dma_start(out[rows, cols], mat_t[g][:, cols])

@@ -34,7 +34,6 @@ def tile_list_tariff_ruling_scores_kernel(
         keep = ctx.enter_context(tc.tile_pool(name="keep", bufs=1))
         ring2 = ctx.enter_context(tc.tile_pool(name="ring2", bufs=2))
         ring3 = ctx.enter_context(tc.tile_pool(name="ring3", bufs=3))
-        ring4 = ctx.enter_context(tc.tile_pool(name="ring4", bufs=4))
         mm = ctx.enter_context(tc.psum_pool(name="mm", bufs=4))
         xs = ctx.enter_context(tc.psum_pool(name="xs", bufs=4))
 
@@ -173,17 +172,6 @@ def tile_list_tariff_ruling_scores_kernel(
 
         h_codes = [keep.tile([P, HALF], U32, name=f"h_c{b}", align_bytes=64) for b in range(2)]
         h_plane = [keep.tile([P, HALF], U8, name=f"h_p{b}", align_bytes=64) for b in range(2)]
-        e_t = [keep.tile([P, S], F32, name=f"e{g}", align_bytes=64) for g in range(GOODS)]
-
-        def scores(g, b):
-            rows = slice(g * P, (g + 1) * P)
-            acc = mm.tile([P, HALF], F32, name="acc")
-            nc.tensor.matmul_mx(
-                out=acc[:], lhsT=v2_w[:, rows].bitcast(FP8X4), lhsT_scale=v2_pl[:, rows],
-                rhs=h_codes[b][:].bitcast(FP8X4), rhs_scale=h_plane[b][:], start=True, stop=True,
-            )
-            nc.scalar.copy(e_t[g][:, b * HALF : (b + 1) * HALF], acc[:])
-
         chan_b = chan_t[:].unsqueeze(1).to_broadcast([P, P, PACK])
         for c in range(CHUNKS):
             acc = product(c, [w_codes["w2", a][:].bitcast(FP8X4) for a in range(PASSES)], [w_plane["w2", a][:] for a in range(PASSES)], (1, 0))
@@ -205,13 +193,28 @@ def tile_list_tariff_ruling_scores_kernel(
             )
 
 
+        def scores(g):
+            rows = slice(g * P, (g + 1) * P)
+            e = ring3.tile([P, S], F32, name="e", align_bytes=64)
+            mx = ring3.tile([P, 2], F32, name="mx")
+            for b in range(2):
+                acc = mm.tile([P, HALF], F32, name="acc")
+                nc.tensor.matmul_mx(
+                    out=acc[:], lhsT=v2_w[:, rows].bitcast(FP8X4), lhsT_scale=v2_pl[:, rows],
+                    rhs=h_codes[b][:].bitcast(FP8X4), rhs_scale=h_plane[b][:], start=True, stop=True,
+                )
+                nc.vector.tensor_scalar(
+                    out=e[:, b * HALF : (b + 1) * HALF], in0=acc[:], scalar1=1.0, scalar2=None,
+                    op0=ALU.mult, op1=ALU.max, accum_out=mx[:, b : b + 1],
+                )
+            nt = ring3.tile([P, 1], F32, name="nt")
+            nc.vector.tensor_scalar(out=nt[:], in0=mx[:, 0:1], scalar1=mx[:, 1:2], scalar2=-1.0, op0=ALU.max, op1=ALU.mult)
+            return e, nt
+
+        ahead = [scores(0), scores(1)]
         for g in range(GOODS):
             rows = slice(g * P, (g + 1) * P)
-            e = e_t[g]
-            scores(g, 0)
-            scores(g, 1)
-            nt = ring4.tile([P, 1], F32, name="nt")
-            nc.vector.tensor_reduce(out=nt[:], in_=e[:], axis=mybir.AxisListType.X, op=ALU.max, negate=True)
+            e, nt = ahead[g]
             a_t = ring3.tile([P, NP], F32, name="a_t", align_bytes=64)
             nc.scalar.activation(out=a_t[:], in_=e[:].indirect(pos1_t[:]), func=ACT.Exp, bias=nt[:])
             nc.scalar.activation(out=a_t[:], in_=a_t[:], func=ACT.Copy, scale=lift_t[:, g : g + 1])
@@ -220,5 +223,8 @@ def tile_list_tariff_ruling_scores_kernel(
             parts = 2 if g == GOODS - 1 else 1
             for part in range(parts):
                 cols = slice(part * NP // parts, (part + 1) * NP // parts)
-                nc.vector.tensor_tensor(mat_t[g][:, cols], c_t[:, cols], mat_t[g][:, cols], ALU.mult)
+                engine = nc.gpsimd if g < GOODS - 2 else nc.vector
+                engine.tensor_tensor(mat_t[g][:, cols], c_t[:, cols], mat_t[g][:, cols], ALU.mult)
                 nc.sync.dma_start(out[rows, cols], mat_t[g][:, cols])
+            if g + 2 < GOODS:
+                ahead.append(scores(g + 2))

from contextlib import ExitStack

import concourse.mybir as mybir
from concourse.masks import make_identity

K, H, T, S, T3, S2, NP = 1024, 512, 4096, 1024, 2048, 1024, 512
FLOPS = 3 * 2 * K * H * S + 2 * H * S2 * S

F32 = mybir.dt.float32
BF16 = mybir.dt.bfloat16
I32 = mybir.dt.int32
U32 = mybir.dt.uint32
U16 = mybir.dt.uint16
U8 = mybir.dt.uint8
FP8X4 = mybir.dt.float8_e4m3fn_x4
FP4X4 = mybir.dt.float4_e2m1fn_x4
ALU = mybir.AluOpType
ACT = mybir.ActivationFunctionType

P = 128
PACK = 4
PASSES = K // (P * PACK)
CHUNKS = S // P
GOODS = S2 // P
HALF = 512


def tile_list_tariff_ruling_scores_kernel(
    tc, tab_words, tab_scales, offs, tab2_words, tab2_scales, offs2, pos1, pos2,
    w1, w2, w3_words, w3_scales, chan, lift, mat, out,
):
    nc = tc.nc
    with ExitStack() as ctx:
        keep = ctx.enter_context(tc.tile_pool(name="keep", bufs=1))
        ring2 = ctx.enter_context(tc.tile_pool(name="ring2", bufs=2))
        ring3 = ctx.enter_context(tc.tile_pool(name="ring3", bufs=3))
        mm = ctx.enter_context(tc.psum_pool(name="mm", bufs=4))
        xs = ctx.enter_context(tc.psum_pool(name="xs", bufs=4))

        offs_t = keep.tile([P, S // 16], U16, name="offs_t")
        offs2_t = keep.tile([P, S2 // 16], U16, name="offs2_t")
        pos1_t = keep.tile([P, NP // 16], U16, name="pos1_t")
        pos2_t = keep.tile([P, NP // 16], U16, name="pos2_t")
        tab_sc = keep.tile([P, PASSES, T], U8, name="tab_sc", align_bytes=64)
        v_sc = keep.tile([P, PASSES, S], U8, name="v_sc", align_bytes=64)
        tab2_sc = keep.tile([P, T3], U8, name="tab2_sc", align_bytes=64)
        tab_w = [keep.tile([P, T], I32, name=f"tab_w{a}", align_bytes=64) for a in range(PASSES)]
        tab2_w = keep.tile([P, T3], I32, name="tab2_w", align_bytes=64)
        w3_w = keep.tile([P, PASSES, 2 * H], U8, name="w3_w", align_bytes=64)
        w3_pl = keep.tile([P, PASSES, H], U8, name="w3_pl", align_bytes=64)
        v_pl = keep.tile([P, PASSES, S], U8, name="v_pl", align_bytes=64)
        v2_pl = keep.tile([P, S2], U8, name="v2_pl", align_bytes=64)
        v2_sc = keep.tile([P, S2], U8, name="v2_sc", align_bytes=64)
        v_w = [keep.tile([P, S], U32, name=f"v_w{a}", align_bytes=64) for a in range(PASSES)]
        v2_w = keep.tile([P, S2], U32, name="v2_w", align_bytes=64)
        ident = keep.tile([P, P], F32, name="ident", align_bytes=64)
        chan_t = keep.tile([P, PACK], F32, name="chan_t")
        lift_t = keep.tile([P, GOODS], F32, name="lift_t")

        SC2 = P - 16
        nc.vector.memset(tab_sc[0:SC2, :, :].rearrange("p a t -> p (a t)").bitcast(I32), 0)
        nc.vector.memset(tab2_sc[0:SC2, :].bitcast(I32), 0)
        nc.gpsimd.memset(w3_pl[:].rearrange("p a c -> p (a c)").bitcast(I32), 0)
        nc.gpsimd.memset(v_pl[:].rearrange("p a t -> p (a t)").bitcast(I32), 0)
        nc.gpsimd.memset(v2_pl[:].bitcast(I32), 0)
        make_identity(nc, ident[:])

        def load_w(w, a, c0, c1, name):
            raw = keep.tile([P, PACK, c1 - c0], F32, name=name, align_bytes=64)
            nc.sync.dma_start(raw[:], w[512 * a : 512 * (a + 1), c0:c1].rearrange("(p i) c -> p i c", i=PACK))
            return raw

        def load_words(a):
            nc.sync.dma_start(tab_w[a][:], tab_words[a].rearrange("p t i -> p (t i)").bitcast(I32))

        def move_rows(plane, gathered):
            for q in range(4):
                nc.sync.dma_start(
                    plane[32 * q : 32 * q + 4, :].bitcast(I32), gathered[SC2 + 4 * q : SC2 + 4 * q + 4, :].bitcast(I32)
                )

        nc.sync.dma_start(offs_t[:], offs)
        nc.sync.dma_start(tab_sc[SC2:P, :, :].bitcast(I32), tab_scales.rearrange("a q t -> q a t").bitcast(I32))
        nc.sync.dma_start(offs2_t[:], offs2)
        nc.sync.dma_start(tab2_sc[SC2:P, :].bitcast(I32), tab2_scales[0].bitcast(I32))
        nc.sync.dma_start(w3_w[:].bitcast(I32), w3_words.rearrange("a p c -> p a c").bitcast(I32))
        load_words(0)
        nc.sync.dma_start(chan_t[:], chan.rearrange("(p i) -> p i", i=PACK))
        nc.sync.dma_start(pos1_t[:], pos1)
        for q in range(4):
            nc.sync.dma_start(
                w3_pl[32 * q : 32 * q + 4, :, :].bitcast(I32),
                w3_scales[:, 4 * q : 4 * q + 4, :].rearrange("a r c -> r a c").bitcast(I32),
            )
        load_words(1)
        for a in range(PASSES):
            nc.vector.tensor_copy(v_sc[:, a, :], tab_sc[:, a, :].indirect(offs_t[:]))
        move_rows(v_pl[:].rearrange("p a t -> p (a t)"), v_sc[:].rearrange("p a t -> p (a t)"))
        w1_raw = [load_w(w1, 0, 0, H, "w1_raw0")]
        w1_raw.append(load_w(w1, 1, 0, H, "w1_raw1"))
        nc.sync.dma_start(tab2_w[:], tab2_words[0].rearrange("p t i -> p (t i)").bitcast(I32))
        w2_raw0 = load_w(w2, 0, 0, H, "w2_raw0")
        w2_raw1 = [load_w(w2, 1, c * 256, (c + 1) * 256, f"w2_raw1_{c}") for c in range(2)]
        nc.vector.tensor_copy(v2_sc[:], tab2_sc[:].indirect(offs2_t[:]))
        move_rows(v2_pl[:], v2_sc[:])
        nc.sync.dma_start(pos2_t[:], pos2)
        with nc.allow_non_contiguous_dma(reason="one value of lift a partition and tile"):
            nc.sync.dma_start(lift_t[:], lift.rearrange("(g p) -> p g", p=P))
        mat_t = []
        for g in range(GOODS):
            m_t = keep.tile([P, NP], F32, name=f"mat{g}", align_bytes=64)
            nc.sync.dma_start(m_t[:], mat[g * P : (g + 1) * P, :])
            mat_t.append(m_t)

        nc.vector.tensor_copy(v_w[0][:], tab_w[0][:].bitcast(U32).indirect(offs_t[:]))
        for hf in range(2):
            nc.vector.tensor_copy(
                v_w[1][:, hf * HALF : (hf + 1) * HALF],
                tab_w[1][:].bitcast(U32).indirect(offs_t[:, hf * 32 : (hf + 1) * 32]),
            )

        def quantise_w(raw, codes, plane, width, copy=nc.vector.tensor_copy):
            grouped = ring2.tile([P, width, PACK], BF16, name="grouped", align_bytes=64)
            copy(
                grouped[:].rearrange("p (c u) i -> p c i u", u=4),
                raw[:].rearrange("p i (c u) -> p c i u", u=4),
            )
            nc.vector.quantize_mx(out=codes.bitcast(FP8X4), scales=plane, in_=grouped[:].rearrange("p c i -> p (c i)"))

        w_codes = {}
        w_plane = {}
        for name in ("w1", "w2"):
            for a in range(PASSES):
                w_codes[name, a] = keep.tile([P, H], U32, name=f"{name}_c{a}", align_bytes=64)
                w_plane[name, a] = keep.tile([P, H], U8, name=f"{name}_p{a}", align_bytes=64)

        def product(c, rhs, rhs_pl, order=(0, 1)):
            acc = mm.tile([P, H], F32, name="acc")
            cols = slice(c * P, (c + 1) * P)
            for a in order:
                nc.tensor.matmul_mx(
                    out=acc[:], lhsT=v_w[a][:, cols].bitcast(FP8X4), lhsT_scale=v_pl[:, a, cols],
                    rhs=rhs[a], rhs_scale=rhs_pl[a], start=(a == order[0]), stop=(a == order[-1]),
                )
            return acc

        def dealt(acc):
            return acc[:].rearrange("j (p i) -> j i p", i=PACK)

        quantise_w(w1_raw[0], w_codes["w1", 0][:], w_plane["w1", 0][:], H)
        r3 = []
        for c in range(CHUNKS):
            acc = product(c, [w3_w[:, a, :].bitcast(FP4X4) for a in range(PASSES)], [w3_pl[:, a, :] for a in range(PASSES)])
            r_sb = keep.tile([P, PACK, P], F32, name=f"r3_{c}", align_bytes=64)
            nc.scalar.copy(r_sb[:], dealt(acc))
            r3.append(r_sb)

        quantise_w(w1_raw[1], w_codes["w1", 1][:], w_plane["w1", 1][:], H)
        nc.vector.tensor_copy(v2_w[:], tab2_w[:].bitcast(U32).indirect(offs2_t[:]))

        r1 = []
        for c in range(CHUNKS):
            acc = product(c, [w_codes["w1", a][:].bitcast(FP8X4) for a in range(PASSES)], [w_plane["w1", a][:] for a in range(PASSES)])
            r_sb = keep.tile([P, PACK, P], F32, name=f"r1_{c}", align_bytes=64)
            nc.scalar.copy(r_sb[:], dealt(acc))
            r1.append(r_sb)

        quantise_w(w2_raw0, w_codes["w2", 0][:], w_plane["w2", 0][:], H)
        for c in range(2):
            cols = slice(c * 256, (c + 1) * 256)
            quantise_w(w2_raw1[c], w_codes["w2", 1][:, cols], w_plane["w2", 1][:, cols], 256)

        h_codes = [keep.tile([P, HALF], U32, name=f"h_c{b}", align_bytes=64) for b in range(2)]
        h_plane = [keep.tile([P, HALF], U8, name=f"h_p{b}", align_bytes=64) for b in range(2)]
        chan_b = chan_t[:].unsqueeze(1).to_broadcast([P, P, PACK])
        for c in range(CHUNKS):
            acc = product(c, [w_codes["w2", a][:].bitcast(FP8X4) for a in range(PASSES)], [w_plane["w2", a][:] for a in range(PASSES)], (1, 0))
            y = ring3.tile([P, PACK, P], F32, name="y", align_bytes=64)
            nc.vector.tensor_tensor(y[:], dealt(acc), r1[c][:], ALU.max)
            x = xs.tile([P, PACK, P], F32, name="x", tag="bank")
            for i in range(PACK):
                nc.tensor.matmul(x[:, i, :], lhsT=r3[c][:, i, :], rhs=ident[:], is_transpose=True, start=(i == 0), stop=False)
            for i in range(PACK):
                nc.tensor.matmul(x[:, i, :], lhsT=y[:, i, :], rhs=ident[:], is_transpose=True, start=False, stop=(i == PACK - 1))
            th = ring3.tile([P, P, PACK], F32, name="th", align_bytes=64)
            nc.scalar.activation(out=th[:], in_=x[:].rearrange("p i j -> p j i"), func=ACT.Tanh)
            hb = ring3.tile([P, P, PACK], BF16, name="hb", align_bytes=64)
            nc.vector.tensor_tensor(hb[:], th[:], chan_b, ALU.mult)
            b, cols = c // 4, slice((c % 4) * P, (c % 4 + 1) * P)
            nc.vector.quantize_mx(
                out=h_codes[b][:, cols].bitcast(FP8X4), scales=h_plane[b][:, cols],
                in_=hb[:].rearrange("p j i -> p (j i)"),
            )


        def scores(g):
            rows = slice(g * P, (g + 1) * P)
            e = ring3.tile([P, S], F32, name="e", align_bytes=64)
            mx = ring3.tile([P, 2], F32, name="mx")
            for b in range(2):
                acc = mm.tile([P, HALF], F32, name="acc")
                nc.tensor.matmul_mx(
                    out=acc[:], lhsT=v2_w[:, rows].bitcast(FP8X4), lhsT_scale=v2_pl[:, rows],
                    rhs=h_codes[b][:].bitcast(FP8X4), rhs_scale=h_plane[b][:], start=True, stop=True,
                )
                nc.vector.tensor_scalar(
                    out=e[:, b * HALF : (b + 1) * HALF], in0=acc[:], scalar1=1.0, scalar2=None,
                    op0=ALU.mult, op1=ALU.max, accum_out=mx[:, b : b + 1],
                )
            nt = ring3.tile([P, 1], F32, name="nt")
            nc.vector.tensor_scalar(out=nt[:], in0=mx[:, 0:1], scalar1=mx[:, 1:2], scalar2=-1.0, op0=ALU.max, op1=ALU.mult)
            return e, nt

        ahead = [scores(0), scores(1)]
        for g in range(GOODS):
            rows = slice(g * P, (g + 1) * P)
            e, nt = ahead[g]
            a_t = ring3.tile([P, NP], F32, name="a_t", align_bytes=64)
            nc.scalar.activation(out=a_t[:], in_=e[:].indirect(pos1_t[:]), func=ACT.Exp, bias=nt[:])
            nc.scalar.activation(out=a_t[:], in_=a_t[:], func=ACT.Copy, scale=lift_t[:, g : g + 1])
            c_t = ring3.tile([P, NP], F32, name="c_t", align_bytes=64)
            nc.vector.tensor_tensor(c_t[:], e[:].indirect(pos2_t[:]), a_t[:], ALU.add)
            parts = 2 if g == GOODS - 1 else 1
            for part in range(parts):
                cols = slice(part * NP // parts, (part + 1) * NP // parts)
                engine = nc.gpsimd if g < GOODS - 2 else nc.vector
                engine.tensor_tensor(mat_t[g][:, cols], c_t[:, cols], mat_t[g][:, cols], ALU.mult)
                nc.sync.dma_start(out[rows, cols], mat_t[g][:, cols])
            if g + 2 < GOODS:
                ahead.append(scores(g + 2))
